import numpy as np
CORES = [88,96,104,112,120,216,224,232,240,248]
N = 10
T, KB = 1024, 16
CAPP = 256
def entries(a): return a.T.reshape(-1)
def pack(v, P): return np.ascontiguousarray(np.asarray(v, np.int32).reshape(-1, P).T)
def order(K):
    return np.argsort(K, kind="stable")
def most(K):
    o = order(K); return int(np.bincount(o // T * N + np.arange(N * T) // T, minlength=N * N).max())
def lists(rng, how):
    i, G = np.arange(N), T // CAPP
    if how == "uniform":
        for again in range(50):
            K = rng.integers(0, KB, (N, T))
            if most(K.reshape(-1)) <= CAPP: break
        else: K = np.broadcast_to(np.arange(T) % KB, (N, T)).copy()
    else:
        if how == "uneven":
            t = rng.integers(0, CAPP + 1, N)
            if t.sum() < T: t = CAPP - t
            t[0] = CAPP; w = np.diff(np.minimum(np.cumsum(t), T), prepend=0); L = w[(rng.permutation(N)[:, None] - rng.permutation(N)) % N]
        else:
            w = np.zeros(N, int); w[(G * (ord(how[-1]) - 97) + np.arange(G)) % N] = CAPP; L = w[(i[:, None] - i) % N]
        a = N - 1 - np.argmax(L[::-1] > 0, axis=0)
        m = np.minimum(rng.integers(1, CAPP, N - 1), L[a[:-1], i[1:]])
        v = np.nonzero((L[a[:-1], i[:-1]] == CAPP) & (L[a[:-1], i[1:]] == CAPP) & (a[:-1] != np.append(-1, a[:-2])))[0]
        if len(v): m[rng.choice(v)] = CAPP
        C = L.copy(); C[a[:-1], i[:-1]] += m; C[a[:-1], i[1:]] -= m
        kv = np.sort(rng.permutation(KB)[:N]); K = np.stack([rng.permutation(np.repeat(kv, c)) for c in C]); K[::3] = np.sort(K[::3], axis=1)
    return {"key": np.stack([pack(k, 16) for k in K])}
def setup_inputs(rng):
    return dict({"x": rng.standard_normal((N, 128, T), dtype=np.float32)}, **lists(rng, "uniform"))
def setup_inputs_fulla(rng):
    d = setup_inputs(rng); d.update(lists(rng, "fulla"))
    for k in ("x",): d[k] = (d[k].astype(np.float32) * 1048576.0).astype(d[k].dtype)
    return d
def setup_inputs_fullb(rng):
    d = setup_inputs(rng); d.update(lists(rng, "fullb"))
    for k in ("x",): d[k] = (d[k].astype(np.float32) * (1 / 1024.0)).astype(d[k].dtype)
    return d
def setup_inputs_fullc(rng):
    d = setup_inputs(rng); d.update(lists(rng, "fullc"))
    return d
def setup_inputs_uneven(rng):
    d = setup_inputs(rng); d.update(lists(rng, "uneven"))
    return d
def check_inputs(x):
    bad = []
    if x["key"].min() < 0 or x["key"].max() >= KB: bad.append("key out of range")
    if most(np.concatenate([entries(a) for a in x["key"]])) > CAPP: bad.append("more than CAPP columns go from one rank to one rank")
    return bad
def reference(x, key):
    X = np.concatenate(list(x), axis=1); K = np.concatenate([entries(a) for a in key])
    Y = X[:, order(K)]
    return {"y": np.stack([Y[:, T * r:T * r + T] for r in range(N)])}

@@ -1,0 +1,390 @@
+import numpy as np
+from concourse.bass import DstId, RemoteDMATransfer
+from concourse.mybir import AluOpType, AxisListType, ActivationFunctionType
+
+WORLD = 256
+NR, NT, CAP = 10, 1024, 256
+NEV = 130
+
+
+def _sb(n, dtype="float32"):
+    return ("sbuf", [128, n], dtype)
+
+
+_SMALL = ["ib", "gnl", "x10", "bs", "mk0", "mk1", "t1", "t2", "t3", "c1", "c2", "qq", "qm0", "qm1", "sg", "sv", "af", "bf"]
+_AT = {n: 32 * k for k, n in enumerate(_SMALL)}
+
+SCRATCH = {
+    "k1": _sb(8, "int32"),
+    "xt": _sb(NT),
+    "xw": _sb(NT + 9 * CAP),
+    "ck": _sb(3 * CAP),
+    "ctl": _sb(4 * NR),
+    "ct": _sb(12),
+    "ci": _sb(64, "int32"), "cf": _sb(10), "l8": _sb(8, "uint16"), "l9": _sb(10, "uint16"),
+    "nf": _sb(144, "int32"), "f7": _sb(144, "int32"), "f15": _sb(144, "int32"), "kk": _sb(128),
+    "geq": _sb(128, "bfloat16"), "nge": _sb(128, "bfloat16"), "mge": _sb(128, "bfloat16"),
+    "mlt": _sb(128, "bfloat16"), "mgt": _sb(128, "bfloat16"), "idn": _sb(128, "bfloat16"),
+    "sel": _sb(8), "bm": _sb(144, "bfloat16"),
+    "lo": _sb(128), "hi": _sb(128), "lo2": _sb(128), "hi2": _sb(128), "dd": _sb(128, "bfloat16"),
+    "oneb": _sb(128, "bfloat16"), "onef": _sb(128), "q15": _sb(128), "trm": _sb(128), "eqm": _sb(128),
+    "xc": _sb(64), "cl": _sb(64), "rl": _sb(64), "c16": _sb(64),
+    "oh": _sb(128, "bfloat16"), "rse": _sb(144, "bfloat16"), "rxx": _sb(144, "bfloat16"),
+    "oht": _sb(128), "zt": _sb(128), "pu": _sb(8, "uint16"), "wb": _sb(NT, "bfloat16"), "sl": _sb(64, "uint16"),
+    "ii": _sb(16), "rc": _sb(64), "lu": _sb(64, "uint16"),
+    "ow": _sb(32 * len(_SMALL)), "oi": _sb(48, "int32"), "ra": _sb(256), "rb": _sb(256), "ll": _sb(512), "yu": _sb(64, "uint16"),
+    "pa": ("psum", [128, 512], "float32"), "pb": ("psum", [128, 512], "float32"), "pc": ("psum", [128, 512], "float32"),
+    "pd": ("psum", [128, 512], "float32"), "pe": ("psum", [128, 512], "float32"), "pf": ("psum", [128, 512], "float32"),
+    "ph": ("psum", [128, 512], "float32"), "pi": ("psum", [128, 512], "float32"),
+}
+SEMAPHORES = ["kin", "xin", "hin", "cin", "pin", "loc", "rep"] + ["e%d" % i for i in range(NEV)]
+
+_CACHE = {}
+
+
+def _make_plan(T, topo):
+    cores = list(T.cores)
+    place = lambda c: (topo.host(c), topo.chip(c))
+    team = []
+    for o in cores:
+        cou = [c for c in range(WORLD) if place(c) == place(o) and c != o
+               and all(topo.may_write(c, d) for d in cores if d != o)]
+        near = [c for c in cou if topo.die(c) == topo.die(o)]
+        far = [c for c in cou if topo.die(c) != topo.die(o)]
+        team.append([o, near[0], far[0], far[1]])
+    mate = [next(m for m in range(WORLD) if topo.mates(o, m)) for o in cores]
+    same = lambda s, d: topo.same_plane(cores[s], cores[d])
+
+    def links(s, d, die):
+        a, b = cores[s], cores[d]
+        if same(s, d):
+            return [("out", place(a), die), ("in", place(b), die)]
+        if topo.mates(a, b):
+            return [("mate", place(a), die)]
+        return [("mate", place(a), die), ("out", place(mate[s]), die), ("in", place(b), die)]
+
+    LK = {(s, d, e): links(s, d, e) for s in range(NR) for d in range(NR) if s != d for e in (0, 1)}
+
+    def cost(A):
+        load = {}
+        for s in range(NR):
+            for d in range(NR):
+                if s != d:
+                    for l in LK[s, d, A[s][d]]:
+                        load[l] = load.get(l, 0) + 1
+        return sum((1.3 if l[0] == "in" else 1.0) * v ** 3 for l, v in load.items())
+
+    def enough(s, row):
+        return sum(1 for d in range(NR) if d != s and row[d] == 0 and same(s, d)) >= 2
+
+    A = []
+    for s in range(NR):
+        near = [d for d in range(NR) if d != s and same(s, d)][:2]
+        near += [d for d in sorted(range(NR), key=lambda d: (3 * d - s) % NR) if d != s and d not in near][:3]
+        A.append([0 if d in near else 1 for d in range(NR)])
+    best, again = cost(A), True
+    while again:
+        again = False
+        for s in range(NR):
+            for d in range(NR):
+                for e in range(NR):
+                    if s in (d, e) or A[s][d] != 0 or A[s][e] != 1:
+                        continue
+                    A[s][d], A[s][e] = 1, 0
+                    c = cost(A) if enough(s, A[s]) else best
+                    if c < best:
+                        best, again = c, True
+                    else:
+                        A[s][d], A[s][e] = 0, 1
+    carry = []
+    for s in range(NR):
+        rot = [(s + k) % NR for k in range(1, NR)]
+        nr = [d for d in rot if A[s][d] == 0]
+        fr = [d for d in rot if A[s][d] == 1]
+        own = [d for d in nr if same(s, d)][:2]
+        carry.append([own, [d for d in nr if d not in own], fr[0::2], fr[1::2]])
+    return {"team": team, "carry": carry}
+
+
+def rank_program(g, core, T, topo):
+    if "plan" not in _CACHE:
+        _CACHE["plan"] = _make_plan(T, topo)
+    plan = _CACHE["plan"]
+    team_of = plan["team"]
+    me = next((r for r in range(NR) if core in team_of[r]), None)
+    if me is None:
+        return
+    team = team_of[me]
+    spot = team.index(core)
+    owner, collect = spot == 0, spot == 1
+    dests = plan["carry"][me][spot]
+    ND = len(dests)
+    NL = 16 * ND + 1
+    OP, AX, COPY = AluOpType, AxisListType.X, ActivationFunctionType.Copy
+    V, S, E = g.vector, g.scalar, g.tensor
+
+    ops = []
+
+    def op(q, fn, deps=(), inc=1):
+        ops.append((q, fn, list(deps), inc))
+        return len(ops) - 1
+
+    def ts(out, in0, s1, op0, s2=None, op1=None, deps=()):
+        if op1 is None:
+            return op("v", lambda: V.tensor_scalar(out=out, in0=in0, scalar1=s1, scalar2=None, op0=op0), deps)
+        return op("v", lambda: V.tensor_scalar(out=out, in0=in0, scalar1=s1, scalar2=s2, op0=op0, op1=op1), deps)
+
+    def tt(out, a, b, o, deps=()):
+        return op("v", lambda: V.tensor_tensor(out=out, in0=a, in1=b, op=o), deps)
+
+    def scan(out, a, b, deps=()):
+        return op("v", lambda: V.tensor_tensor_scan(out=out, data0=a, data1=b, initial=0.0, op0=OP.mult, op1=OP.add), deps)
+
+    def cp(out, a, deps=()):
+        return op("v", lambda: V.tensor_copy(out=out, in_=a), deps)
+
+    def ac(out, a, deps=()):
+        return op("s", lambda: S.activation(out=out, in_=a, func=COPY), deps)
+
+    def ms(a, v, deps=()):
+        return op("v", lambda: V.memset(a, v), deps)
+
+    def red(out, a, deps=()):
+        return op("v", lambda: V.tensor_reduce(out=out, in_=a, axis=AX, op=OP.add), deps)
+
+    def mm(out, l, r, start, stop, deps=()):
+        return op("t", lambda: E.matmul(out=out, lhsT=l, rhs=r, start=start, stop=stop), deps)
+
+    def iota(out, pattern, base, mult, small=False):
+        if small:
+            return op("g", lambda: g.iota(out, pattern, base, mult, allow_small_or_imprecise_dtypes=True))
+        return op("g", lambda: g.iota(out, pattern, base, mult))
+
+    def ow(name, a, b, k=128):
+        return T.ow[0:k, _AT[name] + a:_AT[name] + b]
+
+    loc, rep = [0], [0]
+
+    def write(targets, src, dst, sem, mask, lsem, count, deps=()):
+        ids = [topo.addr(t, core) for t in targets]
+        count[0] += bin(mask).count("1")
+        if len(targets) == 1:
+            rid, pid = ids[0]
+            return op("g", lambda: g.remote_dma(out_ap=dst, in_ap=src, remote_sem=sem, local_sem=lsem, pid=pid, routing_id=rid,
+                                                dma_engine_mask=mask), deps, 0)
+        tr = [RemoteDMATransfer(dst_ids=[DstId(rid=r, pnc=p) for r, p in ids], dma_engine_mask=mask, remote_sem=sem,
+                                srcs=[src], dsts=[dst] * len(targets))]
+        return op("g", lambda: g.remote_dma_fused(tr, local_sem=lsem), deps, 0)
+
+    off = topo.mask(team[1], next(c for c in T.cores if c != team[0]))
+    noff = bin(off).count("1")
+
+    if owner:
+        k_in = op("y", lambda: g.sync.dma_start(T.k1[:], T.key[:]), (), 16)
+        x_in = op("y", lambda: g.sync.dma_start(T.xt[:], T.x[:]), (), 16)
+    else:
+        k_in, x_in = ("kin", noff), ("xin", bin(topo.mask(team[0], core)).count("1"))
+
+    i_p = iota(T.ci[:, 0:1], [[1, 1]], 0, 1)
+    i_8 = iota(T.ci[:, 8:16], [[0, 8]], 0, 1)
+    i_kk = iota(T.kk[:], [[1, 16], [0, 8]], 0, 0, True)
+    i_nf = iota(T.nf[:], [[1, 144]], 0, 0)
+    i_9 = iota(T.ci[:, 24:33], [[16, 9]], 7, 0)
+    if owner:
+        write(team[1:], T.k1[:], T.k1[:], T.sem.kin, off, T.sem.loc, loc, [k_in])
+    i_lo = iota(T.lo[:], [[16, 8], [1, 2], [0, 8]], 0, 0, True)
+    i_hi = iota(T.hi[:], [[0, 16], [128, 8]], 0, 0, True)
+    i_cl = iota(T.cl[:, 0:16 * ND], [[0, ND], [16, 16]], 0, 0, True)
+    if owner:
+        for h in team[1:]:
+            write([h], T.xt[:], T.xt[:], T.sem.xin, topo.mask(core, h), T.sem.rep, rep, [x_in])
+
+    m_one = ms(T.oneb[:], 1.0)
+    m_rse = ms(T.rse[:], 0.0)
+    m_w = ms(T.wb[:], 0.0)
+    m_ii = ms(T.ii[:, 0:1], 0.0)
+    m_ct = ms(T.ct[:, 10:12], 0.0) if collect else None
+    l8i = ts(T.ci[:, 16:24], T.ci[:, 8:16], 7, OP.bitwise_and, deps=[i_8])
+    l8 = cp(T.l8[:], T.ci[:, 16:24], [l8i])
+    c1 = ts(T.ci[:, 1:2], T.ci[:, 0:1], 7, OP.bitwise_and, deps=[i_p])
+    c2 = ts(T.ci[:, 2:3], T.ci[:, 0:1], 15, OP.bitwise_and)
+    c3 = ts(T.ci[:, 3:4], T.ci[:, 0:1], 3, OP.logical_shift_right)
+    c4 = ts(T.ci[:, 4:5], T.ci[:, 0:1], 8, OP.bitwise_and)
+    c5 = ts(T.ci[:, 5:6], T.ci[:, 0:1], 4, OP.logical_shift_right)
+    cf = cp(T.cf[:, 0:6], T.ci[:, 0:6], [c1, c2, c3, c4, c5])
+    PC, GC, QC, KC, EC, RC, M0, M1, RC8 = [T.cf[:, j:j + 1] for j in range(9)]
+    f7 = ts(T.f7[:], T.nf[:], 7, OP.bitwise_and, deps=[i_nf])
+    f15 = ts(T.f15[:], T.nf[:], 15, OP.bitwise_and)
+    F7, F15 = T.f7[:, 0:128], T.f15[:, 0:128]
+
+    def one_hot():
+        return op("v", lambda: V.tensor_tensor(out=T.oh[:], in0=T.k1[:, 0:8].indirect(T.l8[:, 0:8]), in1=T.kk[:], op=OP.is_equal),
+                  [k_in, l8, i_kk])
+
+    if not owner:
+        oh = one_hot()
+        p = mm(T.pa[:, 0:1], T.oh[:], T.oneb[:, 0:1], True, True, [oh, m_one])
+        hist = cp(T.ctl[:, 4 * me:4 * me + 1], T.pa[:, 0:1], [p])
+        rot = [(me + k) % NR for k in range(1, NR)]
+        write([team_of[d][1] for d in rot[spot - 1::3]], T.ctl[:, 4 * me:4 * me + 1], T.ctl[:, 4 * me:4 * me + 1], T.sem.hin, off,
+              T.sem.loc, loc, [hist])
+
+    geq = ts(T.geq[:], F7, GC, OP.is_equal, deps=[f7, cf])
+    nge = ts(T.nge[:], T.nf[:, 0:128], PC, OP.is_le, -1.0, OP.mult)
+    mlt = ts(T.mlt[:], F7, GC, OP.is_gt)
+    mgt = ts(T.mgt[:], F7, GC, OP.is_lt)
+    idn = ts(T.idn[:], T.nf[:, 0:128], PC, OP.is_equal)
+    mge = tt(T.mge[:], T.geq[:], T.nge[:], OP.mult, [geq, nge])
+    l9 = ts(T.l9[:, 0:9], T.ci[:, 24:33], EC, OP.add, deps=[i_9, cf])
+    sel = ts(T.sel[:], T.f7[:, 0:8], GC, OP.is_equal)
+    m0 = ts(M0, QC, 0.0, OP.is_equal)
+    m1 = ts(M1, QC, 1.0, OP.is_equal)
+    bm = ts(T.bm[:], T.f15[:], 0.0, OP.is_equal, deps=[f15])
+    if owner:
+        oh = one_hot()
+    rs = scan(T.rse[:, 8:136], T.oneb[:], T.oh[:], [oh, m_one, m_rse])
+    rx = cp(T.rxx[:], T.rse[:, 0:144].indirect(T.l9[:, 0:9]), [rs, l9])
+    lo2 = ts(T.lo2[:], T.lo[:], KC, OP.add, M0, OP.mult, deps=[i_lo, m0])
+    hi2 = ts(T.hi2[:], T.hi[:], M1, OP.mult, deps=[i_hi, m1])
+    dd = tt(T.dd[:], T.lo2[:], T.hi2[:], OP.add, [lo2, hi2])
+    po = mm(T.pb[:, 0:128], T.oh[:], T.idn[:], True, True, [oh, idn])
+    oht = ac(T.oht[:], T.pb[:, 0:128], [po])
+    mm(T.pc[:, 0:128], T.oh[:], T.mge[:], True, False, [mge])
+    mm(T.pc[:, 0:128], T.rse[:, 8:136], T.geq[:], False, False, [rs, geq])
+    mm(T.pc[:, 0:128], T.rxx[:, 8:136], T.mlt[:], False, False, [rx, mlt])
+    p = mm(T.pc[:, 0:128], T.rxx[:, 0:128], T.mgt[:], False, True, [mgt])
+    z = tt(T.zt[:], T.pc[:, 0:128], T.oht[:], OP.mult, [p, oht])
+    p = mm(T.pd[:, 0:8], T.zt[:], T.sel[:], True, True, [z, sel])
+    pu = cp(T.pu[:], T.pd[:, 0:8], [p])
+    sc = cp(T.wb[:, 0:NT].indirect(T.pu[:, 0:8]), T.dd[:], [pu, m_w, dd])
+    for i in range(16):
+        p = mm(T.pe[:, 0:64], T.bm[:, 16 - i:144 - i], T.wb[:, i:NT:16], i == 0, i == 15, [sc, bm])
+    w = 128 if owner else 16
+    onef = ms(T.onef[:], 1.0)
+    trm = ts(T.trm[:, 0:w], T.f15[:, 0:w], KC, OP.is_gt)
+    eqm = ts(T.eqm[:, 0:w], T.f15[:, 0:w], KC, OP.is_equal)
+    q15 = cp(T.q15[:], F15, [f15])
+    xc = [ms(T.xc[:, 16 * b:16 * b + 16], float(NT * d)) for b, d in enumerate(dests)]
+    xc.append(ms(T.xc[:, NL - 1:NL], 0.0))
+    cl = ms(T.cl[:, NL - 1:NL], 0.0)
+    r1 = ms(T.rl[:, 0:NL - 1], 1.0)
+    r2 = ms(T.rl[:, NL - 1:NL], 0.0)
+    sl = cp(T.sl[:], T.pe[:, 0:64], [p])
+
+    def sort_v():
+        return cp(T.xw[:, 0:512], T.xt[:, 0:NT].indirect(T.sl[:, 0:32]), [sl, x_in])
+
+    if collect:
+        ct = [op("s", lambda: S.activation(out=T.ct[:, 0:10], in_=T.ctl[:, 0:4 * NR:4], func=COPY), [("hin", (NR - 1) * noff), hist]), m_ct]
+        write([team[0], team[2], team[3]], T.ct[:], T.ct[:], T.sem.cin, off, T.sem.loc, loc, ct)
+    else:
+        ct = [("cin", noff)]
+    xs_s = ac(T.xw[:, 512:1024], T.xt[:, 0:NT].indirect(T.sl[:, 32:64]), [sl, x_in])
+    xs_v = sort_v() if owner else None
+    mm(T.ph[:, 0:NL], T.onef[0:1, 0:128], T.cl[0:1, 0:NL], True, False, [onef, i_cl, cl])
+    mm(T.ph[:, 0:NL], T.q15[0:1, 0:128], T.rl[0:1, 0:NL], False, False, [q15, r1, r2])
+    si = scan(T.ii[:, 1:13], T.onef[:, 0:12], T.ct[:, 0:12], ct + [onef, m_ii])
+    mm(T.pf[0:16, 0:2], T.trm[:, 0:16], T.ii[:, 11:13], True, False, [si, trm])
+    p = mm(T.pf[0:16, 0:2], T.eqm[:, 0:16], T.ii[:, me:me + 2], False, True, [eqm, m_ii])
+    rc = ts(T.rc[0:16, 0:NL], T.xc[0:16, 0:NL], T.pf[0:16, 1:2], OP.min, T.pf[0:16, 0:1], OP.max, deps=[p] + xc)
+    p = mm(T.ph[:, 0:NL], T.onef[0:16, 0:128], T.rc[0:16, 0:NL], False, True, [rc])
+    lu = ts(T.lu[:, 0:NL - 1], T.ph[:, 0:NL - 1], T.ph[:, NL - 1:NL], OP.subtract, float(NT - 1), OP.min, deps=[p])
+    if not owner:
+        xs_v = sort_v()
+    for b, d in enumerate(dests):
+        out, win = T.ck[:, CAP * b:CAP * b + CAP], T.xw[:, 0:NT].indirect(T.lu[:, 16 * b:16 * b + 16])
+        c = (cp if b % 2 == 0 else ac)(out, win, [lu, xs_v, xs_s])
+        slot = NT + CAP * (me if me < d else me - 1)
+        write([team_of[d][0]], out, T.xw[:, slot:slot + CAP], T.sem.pin, off, T.sem.loc, loc, [c])
+
+    if owner:
+        RI, UI, AI, BI = T.oi[:, 0:30], T.oi[:, 32:36], T.oi[:, 36:40], T.oi[:, 40:44]
+        i_ri = iota(RI, [[0, 3], [1, 10]], 0, 0)
+        i_16 = iota(T.c16[:], [[16, 64]], 0, 0, True)
+        ib_ = []
+        if me > 0:
+            ib_.append(iota(ow("bs", 0, me), [[CAP, me]], NT + NT * me, 0, True))
+        if me < NR - 1:
+            ib_.append(iota(ow("bs", me + 1, NR), [[CAP, NR - 1 - me]], NT + NT * me + CAP * me, 0, True))
+        kb = ms(ow("bs", me, me + 1), float(NT * me))
+        ka = ms(ow("x10", 0, 10), float(NT * me))
+        kx = ms(ow("x10", me, me + 1), 0.0, [ka])
+        r8 = ts(RC8, RC, 8.0, OP.add)
+        k0 = ts(ow("mk0", 0, 30), RI, RC, OP.is_equal, deps=[i_ri])
+        k1 = ts(ow("mk1", 0, 30), RI, RC8, OP.is_equal, deps=[r8])
+        ib = ts(ow("ib", 0, 10), T.onef[:, 0:10], T.ii[:, 10:11], OP.mult, deps=[si])
+        mm(T.pa[:, 0:10], T.trm[:], ow("ib", 0, 10), True, False, [ib])
+        mm(T.pa[:, 0:10], T.eqm[:], T.ii[:, 0:10], False, True)
+        mm(T.pa[:, 10:20], T.eqm[:], T.ct[:, 0:10], True, True, ct)
+        p = mm(T.pa[:, 20:30], T.trm[:], T.ct[:, 0:10], True, True)
+        gn = cp(ow("gnl", 0, 30), T.pa[:, 0:30], [p])
+        G, NN, L = ow("gnl", 0, 10), ow("gnl", 10, 20), ow("gnl", 20, 30)
+        t1 = tt(ow("t1", 0, 10), ow("x10", 0, 10), G, OP.subtract, [gn, kx])
+        c1 = tt(ow("c1", 0, 10), L, G, OP.subtract)
+        t2 = tt(ow("t2", 0, 10), ow("t1", 0, 10), NN, OP.min, [t1])
+        q0 = cp(ow("qq", 0, 10), G)
+        t3 = ts(ow("t3", 0, 10), ow("t2", 0, 10), 0.0, OP.max, deps=[t2])
+        q1 = tt(ow("qq", 10, 20), G, NN, OP.add)
+        c2 = tt(ow("c2", 0, 10), ow("c1", 0, 10), ow("bs", 0, 10), OP.add, [c1, kb] + ib_)
+        p = mm(T.pb[:, 0:10], T.onef[0:16, 0:128], ow("t3", 0, 10, 16), True, True, [t3])
+        q2 = tt(ow("qq", 20, 30), ow("c2", 0, 10), T.pb[:, 0:10], OP.subtract, [p, c2])
+        a0 = tt(ow("qm0", 0, 30), ow("qq", 0, 30), ow("mk0", 0, 30), OP.mult, [q0, q1, q2, k0])
+        a1 = tt(ow("qm1", 0, 30), ow("qq", 0, 30), ow("mk1", 0, 30), OP.mult, [k1])
+        r = []
+        for s, qm, a in ((0, "qm0", a0), (1, "qm1", a1)):
+            r.append(red(ow("sg", 2 * s, 2 * s + 1), ow(qm, 0, 10), [a]))
+            r.append(red(ow("sg", 2 * s + 1, 2 * s + 2), ow(qm, 10, 20)))
+            r.append(red(ow("sv", 2 * s, 2 * s + 1), ow(qm, 20, 30)))
+        u = ts(UI, ow("sg", 0, 4), float(NT * me), OP.subtract, deps=r)
+        n = [ts(ow("sv", 2 * s + 1, 2 * s + 2), ow("sv", 2 * s, 2 * s + 1), -1.0, OP.mult) for s in (0, 1)]
+        ai = ts(AI, UI, 4, OP.arith_shift_right, deps=[u])
+        bi = ts(BI, UI, 15, OP.bitwise_and)
+        af = cp(ow("af", 0, 4), AI, [ai])
+        bf = cp(ow("bf", 0, 4), BI, [bi])
+        mm(T.pi[:, 0:64], T.onef[0:1, 0:128], T.c16[0:1, 0:64], True, False, [i_16])
+        mm(T.pi[:, 0:64], T.q15[0:1, 0:128], T.onef[0:1, 0:64], False, False)
+        for s, e in ((0, 0), (0, 1), (1, 0), (1, 1)):
+            K, o = (128, 32)[s], 2 * s + e
+            A, B, C = [ow(b, o, o + 1, K) for b in ("af", "bf", "sv")]
+            R1, R2, LL = T.ra[0:K, 64 * o:64 * o + 64], T.rb[0:K, 64 * o:64 * o + 64], T.ll[0:K, 128 * o:128 * o + 128]
+            v1 = ts(R1, T.nf[0:K, 0:64], A, OP.is_gt, C, OP.mult, deps=[af, bf] + n)
+            v2 = ts(R2, T.nf[0:K, 0:64], A, OP.is_equal, C, OP.mult)
+            v3 = ts(LL, T.f15[0:K, 0:128], B, OP.is_ge)
+            mm(T.pi[:, 0:64], T.onef[0:K, 0:128], R1, False, False, [v1])
+            p = mm(T.pi[:, 0:64], LL, R2, False, (s, e) == (1, 1), [v2, v3])
+        yu = cp(T.yu[:], T.pi[:, 0:64], [p])
+        ready = [yu, xs_v, xs_s, ("pin", (NR - 1) * noff), ("rep", rep[0])]
+        pc = {}
+        for b, f in ((0, cp), (2, ac), (1, cp), (3, ac)):
+            pc[b] = f(T.xt[:, CAP * b:CAP * b + CAP], T.xw[:, 0:NT + 9 * CAP].indirect(T.yu[:, 16 * b:16 * b + 16]), ready)
+        for b, q in ((0, "y"), (2, "y"), (1, "y"), (3, "s")):
+            eng = g.sync if q == "y" else g.scalar
+            op(q, lambda eng=eng, b=b: eng.dma_start(T.y[:, CAP * b:CAP * b + CAP], T.xt[:, CAP * b:CAP * b + CAP]), [pc[b]], 16)
+
+    queue = {"g": g, "v": V, "t": E, "s": S, "y": g.sync}
+    needed = set(d for o in ops for d in o[2] if isinstance(d, int)) | set(i for i, o in enumerate(ops) if o[3] == 16)
+    event, seen, waited = {}, {q: set() for q in queue}, set()
+
+    def wait(q, d):
+        if d in seen[q]:
+            return
+        seen[q].add(d)
+        waited.add(d)
+        if isinstance(d, int):
+            queue[q].wait_ge(event[d][0], event[d][1])
+        else:
+            queue[q].wait_ge(T.sem[d[0]], d[1])
+
+    for i, (q, fn, deps, inc) in enumerate(ops):
+        for d in deps:
+            wait(q, d)
+        ins = fn()
+        if i in needed:
+            event[i] = (T.sem["e%d" % len(event)], inc)
+            ins.then_inc(event[i][0], inc)
+    for i in sorted(event):
+        if i not in waited:
+            wait("g", i)
+    wait("g", ("loc", loc[0]))
+    if owner:
+        wait("g", ("rep", rep[0]))

@@ -4,40 +4,48 @@ from concourse.mybir import AluOpType, AxisListType, ActivationFunctionType
 
 WORLD = 256
 NR, NT, CAP = 10, 1024, 256
-NEV = 130
+NEV = 141
 
 
 def _sb(n, dtype="float32"):
     return ("sbuf", [128, n], dtype)
 
 
-_SMALL = ["ib", "gnl", "x10", "bs", "mk0", "mk1", "t1", "t2", "t3", "c1", "c2", "qq", "qm0", "qm1", "sg", "sv", "af", "bf"]
+_SMALL = ["bs", "e0", "e1", "e2", "wa", "wb", "mi", "gs", "sg", "sv", "bf"]
 _AT = {n: 32 * k for k, n in enumerate(_SMALL)}
+COLLECT = (1, 2)
+HAND = ((0, 1), (3, 2))
+SHARE = (0, 7, 13, 18)
+SLOTS = [(0, 0), (0, 1), (1, 0), (1, 1), (1, 2), (2, 0), (2, 1), (3, 0), (3, 1)]
+LATE = (1.6, 0.0, 0.1, 1.6)
+OWN, CUT = 2, 4
+PIECES = (("v", 128), ("s", 128), ("v", 384), ("s", 384))
 
 SCRATCH = {
     "k1": _sb(8, "int32"),
     "xt": _sb(NT),
     "xw": _sb(NT + 9 * CAP),
     "ck": _sb(3 * CAP),
-    "ctl": _sb(4 * NR),
-    "ct": _sb(12),
+    "hs": _sb(8, "bfloat16"),
+    "ctl": _sb(80, "bfloat16"),
     "ci": _sb(64, "int32"), "cf": _sb(10), "l8": _sb(8, "uint16"), "l9": _sb(10, "uint16"),
     "nf": _sb(144, "int32"), "f7": _sb(144, "int32"), "f15": _sb(144, "int32"), "kk": _sb(128),
     "geq": _sb(128, "bfloat16"), "nge": _sb(128, "bfloat16"), "mge": _sb(128, "bfloat16"),
     "mlt": _sb(128, "bfloat16"), "mgt": _sb(128, "bfloat16"), "idn": _sb(128, "bfloat16"),
     "sel": _sb(8), "bm": _sb(144, "bfloat16"),
-    "lo": _sb(128), "hi": _sb(128), "lo2": _sb(128), "hi2": _sb(128), "dd": _sb(128, "bfloat16"),
-    "oneb": _sb(128, "bfloat16"), "onef": _sb(128), "q15": _sb(128), "trm": _sb(128), "eqm": _sb(128),
-    "xc": _sb(64), "cl": _sb(64), "rl": _sb(64), "c16": _sb(64),
+    "lo": _sb(128), "lo2": _sb(128), "hi2": _sb(128), "dd": _sb(128, "bfloat16"), "zb": _sb(256, "bfloat16"),
+    "oneb": _sb(128, "bfloat16"), "onef": _sb(128), "q15": _sb(128), "trm": _sb(128, "bfloat16"), "eqm": _sb(128, "bfloat16"),
+    "xc": _sb(64), "cl": _sb(64), "rl": _sb(64), "c16": _sb(144),
     "oh": _sb(128, "bfloat16"), "rse": _sb(144, "bfloat16"), "rxx": _sb(144, "bfloat16"),
     "oht": _sb(128), "zt": _sb(128), "pu": _sb(8, "uint16"), "wb": _sb(NT, "bfloat16"), "sl": _sb(64, "uint16"),
-    "ii": _sb(16), "rc": _sb(64), "lu": _sb(64, "uint16"),
-    "ow": _sb(32 * len(_SMALL)), "oi": _sb(48, "int32"), "ra": _sb(256), "rb": _sb(256), "ll": _sb(512), "yu": _sb(64, "uint16"),
+    "gx": _sb(32), "rc": _sb(64), "lu": _sb(64, "uint16"),
+    "ow": _sb(32 * len(_SMALL)), "oi": _sb(48, "int32"), "md": _sb(96), "mg": _sb(32), "pr": _sb(96), "ra": _sb(256), "ll": _sb(512),
+    "yu": _sb(64, "uint16"),
     "pa": ("psum", [128, 512], "float32"), "pb": ("psum", [128, 512], "float32"), "pc": ("psum", [128, 512], "float32"),
     "pd": ("psum", [128, 512], "float32"), "pe": ("psum", [128, 512], "float32"), "pf": ("psum", [128, 512], "float32"),
     "ph": ("psum", [128, 512], "float32"), "pi": ("psum", [128, 512], "float32"),
 }
-SEMAPHORES = ["kin", "xin", "hin", "cin", "pin", "loc", "rep"] + ["e%d" % i for i in range(NEV)]
+SEMAPHORES = ["kin", "xin", "hin", "cin", "pin", "cst", "loc", "rep"] + ["e%d" % i for i in range(NEV)]
 
 _CACHE = {}
 
@@ -64,46 +72,63 @@ def _make_plan(T, topo):
         return [("mate", place(a), die), ("out", place(mate[s]), die), ("in", place(b), die)]
 
     LK = {(s, d, e): links(s, d, e) for s in range(NR) for d in range(NR) if s != d for e in (0, 1)}
+    TIME = {"out": 0.85, "in": 1.0, "mate": 1.0}
+    start = [LATE[c] + 0.25 * i for c, i in SLOTS]
+    seq = sorted(range(9), key=lambda p: start[p])
+    alone = [d for d in range(NR) if not any(topo.mates(cores[d], c) for c in cores)]
 
-    def cost(A):
-        load = {}
+    def cost(B, half):
+        free, last = {}, [0.0] * NR
+        for p in seq:
+            for s in range(NR):
+                d = B[s][p]
+                parts = [(start[p], SLOTS[p][0], 1.0)]
+                if p == CUT and half.get(d) == s:
+                    parts = [(start[p], 1, 0.5), (start[p] + 0.25, 2, 0.5)]
+                for st, c, z in parts:
+                    end = free[s, c] = max(free.get((s, c), 0.0), st) + 0.9 * z
+                    for l in LK[s, d, 0 if c < 2 else 1]:
+                        free[l] = max(free.get(l, 0.0), st) + TIME[l[0]] * z
+                        end = max(end, free[l])
+                    last[d] = max(last[d], end)
+        return sum(t ** 16 for t in free.values()) + sum(t ** 16 for t in last)
+
+    def fits(s, row, half):
+        return all(same(s, d) for d in row[:OWN]) and all(row[CUT] == d for d in half if half[d] == s)
+
+    best = None
+    for shift in range(8):
+        half = {d: (d + 1 + shift) % NR for d in alone}
+        B = []
         for s in range(NR):
-            for d in range(NR):
-                if s != d:
-                    for l in LK[s, d, A[s][d]]:
-                        load[l] = load.get(l, 0) + 1
-        return sum((1.3 if l[0] == "in" else 1.0) * v ** 3 for l, v in load.items())
-
-    def enough(s, row):
-        return sum(1 for d in range(NR) if d != s and row[d] == 0 and same(s, d)) >= 2
-
-    A = []
-    for s in range(NR):
-        near = [d for d in range(NR) if d != s and same(s, d)][:2]
-        near += [d for d in sorted(range(NR), key=lambda d: (3 * d - s) % NR) if d != s and d not in near][:3]
-        A.append([0 if d in near else 1 for d in range(NR)])
-    best, again = cost(A), True
-    while again:
-        again = False
-        for s in range(NR):
-            for d in range(NR):
-                for e in range(NR):
-                    if s in (d, e) or A[s][d] != 0 or A[s][e] != 1:
-                        continue
-                    A[s][d], A[s][e] = 1, 0
-                    c = cost(A) if enough(s, A[s]) else best
-                    if c < best:
-                        best, again = c, True
-                    else:
-                        A[s][d], A[s][e] = 0, 1
+            rot = [(s + k) % NR for k in range(1, NR)]
+            cut = [d for d in rot if half.get(d) == s]
+            own = [d for d in rot if same(s, d) and d not in cut][:OWN]
+            row = own + [d for d in rot if d not in own + cut]
+            B.append(row[:CUT] + cut + row[CUT:])
+        now, again = cost(B, half), True
+        while again:
+            again = False
+            for s in range(NR):
+                row = B[s]
+                for p in range(9):
+                    for q in range(p + 1, 9):
+                        row[p], row[q] = row[q], row[p]
+                        c = cost(B, half) if fits(s, row, half) else now
+                        if c < now:
+                            now, again = c, True
+                        else:
+                            row[p], row[q] = row[q], row[p]
+        if best is None or now < best[0]:
+            best = (now, [list(row) for row in B], half)
+    half = best[2]
     carry = []
-    for s in range(NR):
-        rot = [(s + k) % NR for k in range(1, NR)]
-        nr = [d for d in rot if A[s][d] == 0]
-        fr = [d for d in rot if A[s][d] == 1]
-        own = [d for d in nr if same(s, d)][:2]
-        carry.append([own, [d for d in nr if d not in own], fr[0::2], fr[1::2]])
-    return {"team": team, "carry": carry}
+    for s, row in enumerate(best[1]):
+        cut = [d for d in half if half[d] == s]
+        c4 = [[(row[p], 0, CAP // 2 if row[p] in cut else CAP) for p in range(9) if SLOTS[p][0] == c] for c in range(4)]
+        c4[2] += [(d, CAP // 2, CAP) for d in cut]
+        carry.append(c4)
+    return {"team": team, "carry": carry, "half": half}
 
 
 def rank_program(g, core, T, topo):
@@ -116,7 +141,7 @@ def rank_program(g, core, T, topo):
         return
     team = team_of[me]
     spot = team.index(core)
-    owner, collect = spot == 0, spot == 1
+    owner, collect = spot == 0, spot in COLLECT
     dests = plan["carry"][me][spot]
     ND = len(dests)
     NL = 16 * ND + 1
@@ -137,8 +162,8 @@ def rank_program(g, core, T, topo):
     def tt(out, a, b, o, deps=()):
         return op("v", lambda: V.tensor_tensor(out=out, in0=a, in1=b, op=o), deps)
 
-    def scan(out, a, b, deps=()):
-        return op("v", lambda: V.tensor_tensor_scan(out=out, data0=a, data1=b, initial=0.0, op0=OP.mult, op1=OP.add), deps)
+    def scan(out, a, b, deps=(), initial=0.0):
+        return op("v", lambda: V.tensor_tensor_scan(out=out, data0=a, data1=b, initial=initial, op0=OP.mult, op1=OP.add), deps)
 
     def cp(out, a, deps=()):
         return op("v", lambda: V.tensor_copy(out=out, in_=a), deps)
@@ -178,75 +203,97 @@ def rank_program(g, core, T, topo):
 
     off = topo.mask(team[1], next(c for c in T.cores if c != team[0]))
     noff = bin(off).count("1")
+    onc = [topo.mask(team[0], h) for h in team[1:]]
+    H = NT // 2
 
     if owner:
         k_in = op("y", lambda: g.sync.dma_start(T.k1[:], T.key[:]), (), 16)
-        x_in = op("y", lambda: g.sync.dma_start(T.xt[:], T.x[:]), (), 16)
+        x_in = [op("y", lambda: g.sync.dma_start(T.xt[:, 0:H], T.x[:, 0:H]), (), 16),
+                op("y", lambda: g.sync.dma_start(T.xt[:, H:NT], T.x[:, H:NT]), (), 16)]
     else:
-        k_in, x_in = ("kin", noff), ("xin", bin(topo.mask(team[0], core)).count("1"))
+        k_in, x_in = ("kin", noff), [("xin", 2 * bin(onc[spot - 1]).count("1"))]
 
     i_p = iota(T.ci[:, 0:1], [[1, 1]], 0, 1)
     i_8 = iota(T.ci[:, 8:16], [[0, 8]], 0, 1)
-    i_kk = iota(T.kk[:], [[1, 16], [0, 8]], 0, 0, True)
     i_nf = iota(T.nf[:], [[1, 144]], 0, 0)
+    i_kk = iota(T.kk[:], [[1, 16], [0, 8]], 0, 0, True)
     i_9 = iota(T.ci[:, 24:33], [[16, 9]], 7, 0)
+    i_lo = iota(T.lo[:], [[16, 8], [1, 2], [0, 8]], 0, 0, True)
     if owner:
         write(team[1:], T.k1[:], T.k1[:], T.sem.kin, off, T.sem.loc, loc, [k_in])
-    i_lo = iota(T.lo[:], [[16, 8], [1, 2], [0, 8]], 0, 0, True)
-    i_hi = iota(T.hi[:], [[0, 16], [128, 8]], 0, 0, True)
+        for h, m in zip(team[1:], onc):
+            for a, xd in ((0, x_in[0]), (H, x_in[1])):
+                write([h], T.xt[:, a:a + H], T.xt[:, a:a + H], T.sem.xin, m, T.sem.rep, rep, [xd])
+    else:
+        tab, pat, base = ((T.oi[:, 0:32], [[1, 32]], -18), (T.c16[:, 0:64], [[16, 64]], 0), (T.c16[:, 64:129], [[16, 65]], NT * me))[spot - 1]
+        write([team[0]], tab, tab, T.sem.cst, off, T.sem.loc, loc, [iota(tab, pat, base, 0, spot > 1)])
     i_cl = iota(T.cl[:, 0:16 * ND], [[0, ND], [16, 16]], 0, 0, True)
     if owner:
-        for h in team[1:]:
-            write([h], T.xt[:], T.xt[:], T.sem.xin, topo.mask(core, h), T.sem.rep, rep, [x_in])
+        i_bs = []
+        if me > 0:
+            i_bs.append(iota(ow("bs", 0, me), [[CAP, me]], NT + NT * me, 0, True))
+        if me < NR - 1:
+            i_bs.append(iota(ow("bs", me + 1, NR), [[CAP, NR - 1 - me]], NT + NT * me + CAP * me, 0, True))
 
     m_one = ms(T.oneb[:], 1.0)
+    m_z = ms(T.zb[:], 0.0)
+    m_w = [ac(T.wb[:, 256 * j:256 * j + 256], T.zb[:], [m_z]) for j in range(4)]
     m_rse = ms(T.rse[:], 0.0)
-    m_w = ms(T.wb[:], 0.0)
-    m_ii = ms(T.ii[:, 0:1], 0.0)
-    m_ct = ms(T.ct[:, 10:12], 0.0) if collect else None
     l8i = ts(T.ci[:, 16:24], T.ci[:, 8:16], 7, OP.bitwise_and, deps=[i_8])
-    l8 = cp(T.l8[:], T.ci[:, 16:24], [l8i])
     c1 = ts(T.ci[:, 1:2], T.ci[:, 0:1], 7, OP.bitwise_and, deps=[i_p])
     c2 = ts(T.ci[:, 2:3], T.ci[:, 0:1], 15, OP.bitwise_and)
     c3 = ts(T.ci[:, 3:4], T.ci[:, 0:1], 3, OP.logical_shift_right)
     c4 = ts(T.ci[:, 4:5], T.ci[:, 0:1], 8, OP.bitwise_and)
     c5 = ts(T.ci[:, 5:6], T.ci[:, 0:1], 4, OP.logical_shift_right)
+    l8 = cp(T.l8[:], T.ci[:, 16:24], [l8i])
     cf = cp(T.cf[:, 0:6], T.ci[:, 0:6], [c1, c2, c3, c4, c5])
-    PC, GC, QC, KC, EC, RC, M0, M1, RC8 = [T.cf[:, j:j + 1] for j in range(9)]
+    PC, GC, QC, KC, EC, RC, M0, M1 = [T.cf[:, j:j + 1] for j in range(8)]
+    m0 = ts(M0, QC, 0.0, OP.is_equal, deps=[cf])
+    m1 = ts(M1, QC, 1.0, OP.is_equal)
     f7 = ts(T.f7[:], T.nf[:], 7, OP.bitwise_and, deps=[i_nf])
     f15 = ts(T.f15[:], T.nf[:], 15, OP.bitwise_and)
     F7, F15 = T.f7[:, 0:128], T.f15[:, 0:128]
+    geq = ts(T.geq[:], F7, GC, OP.is_equal, deps=[f7])
+    nge = ts(T.nge[:], T.nf[:, 0:128], PC, OP.is_le, -1.0, OP.mult)
+    l9 = ts(T.l9[:, 0:9], T.ci[:, 24:33], EC, OP.add, deps=[i_9])
 
     def one_hot():
         return op("v", lambda: V.tensor_tensor(out=T.oh[:], in0=T.k1[:, 0:8].indirect(T.l8[:, 0:8]), in1=T.kk[:], op=OP.is_equal),
                   [k_in, l8, i_kk])
 
-    if not owner:
-        oh = one_hot()
-        p = mm(T.pa[:, 0:1], T.oh[:], T.oneb[:, 0:1], True, True, [oh, m_one])
-        hist = cp(T.ctl[:, 4 * me:4 * me + 1], T.pa[:, 0:1], [p])
-        rot = [(me + k) % NR for k in range(1, NR)]
-        write([team_of[d][1] for d in rot[spot - 1::3]], T.ctl[:, 4 * me:4 * me + 1], T.ctl[:, 4 * me:4 * me + 1], T.sem.hin, off,
-              T.sem.loc, loc, [hist])
+    def sort_constants():
+        mlt = ts(T.mlt[:], F7, GC, OP.is_gt)
+        mgt = ts(T.mgt[:], F7, GC, OP.is_lt)
+        idn = ts(T.idn[:], T.nf[:, 0:128], PC, OP.is_equal)
+        mge = tt(T.mge[:], T.geq[:], T.nge[:], OP.mult, [geq, nge])
+        sel = ts(T.sel[:], T.f7[:, 0:8], GC, OP.is_equal)
+        return mlt, mgt, idn, mge, sel
 
-    geq = ts(T.geq[:], F7, GC, OP.is_equal, deps=[f7, cf])
-    nge = ts(T.nge[:], T.nf[:, 0:128], PC, OP.is_le, -1.0, OP.mult)
-    mlt = ts(T.mlt[:], F7, GC, OP.is_gt)
-    mgt = ts(T.mgt[:], F7, GC, OP.is_lt)
-    idn = ts(T.idn[:], T.nf[:, 0:128], PC, OP.is_equal)
-    mge = tt(T.mge[:], T.geq[:], T.nge[:], OP.mult, [geq, nge])
-    l9 = ts(T.l9[:, 0:9], T.ci[:, 24:33], EC, OP.add, deps=[i_9, cf])
-    sel = ts(T.sel[:], T.f7[:, 0:8], GC, OP.is_equal)
-    m0 = ts(M0, QC, 0.0, OP.is_equal)
-    m1 = ts(M1, QC, 1.0, OP.is_equal)
-    bm = ts(T.bm[:], T.f15[:], 0.0, OP.is_equal, deps=[f15])
+    def scatter_constants():
+        bm = ts(T.bm[:], T.f15[:], 0.0, OP.is_equal, deps=[f15])
+        hi2 = ts(T.hi2[:], F7, M1, OP.mult, 128.0, OP.mult, deps=[m1])
+        lo2 = ts(T.lo2[:], T.lo[:], KC, OP.add, M0, OP.mult, deps=[i_lo, m0])
+        dd = tt(T.dd[:], T.lo2[:], T.hi2[:], OP.add, [lo2, hi2])
+        return bm, dd
+
     if owner:
         oh = one_hot()
+        mlt, mgt, idn, mge, sel = sort_constants()
+    else:
+        mlt, mgt, idn, mge, sel = sort_constants()
+        bm, dd = scatter_constants()
+        oh = one_hot()
+        p = mm(T.pa[:, 0:8], T.oh[:], T.oneb[:, 0:8], True, True, [oh, m_one])
+        hist = cp(T.hs[:], T.pa[:, 0:8], [p])
+        cols = [((me + k) % NR, c) for k in range(1, NR) for c in COLLECT]
+        write([team_of[d][c] for d, c in cols[SHARE[spot - 1]:SHARE[spot]]], T.hs[:], T.ctl[:, 8 * me:8 * me + 8], T.sem.hin, off,
+              T.sem.loc, loc, [hist])
+
     rs = scan(T.rse[:, 8:136], T.oneb[:], T.oh[:], [oh, m_one, m_rse])
+    own_ct = [cp(T.ctl[:, 8 * me:8 * me + 8], T.hs[:], [hist])] if collect else []
     rx = cp(T.rxx[:], T.rse[:, 0:144].indirect(T.l9[:, 0:9]), [rs, l9])
-    lo2 = ts(T.lo2[:], T.lo[:], KC, OP.add, M0, OP.mult, deps=[i_lo, m0])
-    hi2 = ts(T.hi2[:], T.hi[:], M1, OP.mult, deps=[i_hi, m1])
-    dd = tt(T.dd[:], T.lo2[:], T.hi2[:], OP.add, [lo2, hi2])
+    if owner:
+        bm, dd = scatter_constants()
     po = mm(T.pb[:, 0:128], T.oh[:], T.idn[:], True, True, [oh, idn])
     oht = ac(T.oht[:], T.pb[:, 0:128], [po])
     mm(T.pc[:, 0:128], T.oh[:], T.mge[:], True, False, [mge])
@@ -256,110 +303,112 @@ def rank_program(g, core, T, topo):
     z = tt(T.zt[:], T.pc[:, 0:128], T.oht[:], OP.mult, [p, oht])
     p = mm(T.pd[:, 0:8], T.zt[:], T.sel[:], True, True, [z, sel])
     pu = cp(T.pu[:], T.pd[:, 0:8], [p])
-    sc = cp(T.wb[:, 0:NT].indirect(T.pu[:, 0:8]), T.dd[:], [pu, m_w, dd])
+    sc = cp(T.wb[:, 0:NT].indirect(T.pu[:, 0:8]), T.dd[:], [pu, dd] + m_w)
     for i in range(16):
         p = mm(T.pe[:, 0:64], T.bm[:, 16 - i:144 - i], T.wb[:, i:NT:16], i == 0, i == 15, [sc, bm])
     w = 128 if owner else 16
     onef = ms(T.onef[:], 1.0)
     trm = ts(T.trm[:, 0:w], T.f15[:, 0:w], KC, OP.is_gt)
     eqm = ts(T.eqm[:, 0:w], T.f15[:, 0:w], KC, OP.is_equal)
-    q15 = cp(T.q15[:], F15, [f15])
-    xc = [ms(T.xc[:, 16 * b:16 * b + 16], float(NT * d)) for b, d in enumerate(dests)]
-    xc.append(ms(T.xc[:, NL - 1:NL], 0.0))
+    q15 = cp(T.q15[:], F15)
+    xc = [ms(T.xc[:, 16 * b:16 * b + 16], float(NT * d)) for b, (d, _, _) in enumerate(dests)] + [ms(T.xc[:, NL - 1:NL], 0.0)]
     cl = ms(T.cl[:, NL - 1:NL], 0.0)
     r1 = ms(T.rl[:, 0:NL - 1], 1.0)
     r2 = ms(T.rl[:, NL - 1:NL], 0.0)
     sl = cp(T.sl[:], T.pe[:, 0:64], [p])
-
-    def sort_v():
-        return cp(T.xw[:, 0:512], T.xt[:, 0:NT].indirect(T.sl[:, 0:32]), [sl, x_in])
-
-    if collect:
-        ct = [op("s", lambda: S.activation(out=T.ct[:, 0:10], in_=T.ctl[:, 0:4 * NR:4], func=COPY), [("hin", (NR - 1) * noff), hist]), m_ct]
-        write([team[0], team[2], team[3]], T.ct[:], T.ct[:], T.sem.cin, off, T.sem.loc, loc, ct)
-    else:
-        ct = [("cin", noff)]
-    xs_s = ac(T.xw[:, 512:1024], T.xt[:, 0:NT].indirect(T.sl[:, 32:64]), [sl, x_in])
-    xs_v = sort_v() if owner else None
-    mm(T.ph[:, 0:NL], T.onef[0:1, 0:128], T.cl[0:1, 0:NL], True, False, [onef, i_cl, cl])
-    mm(T.ph[:, 0:NL], T.q15[0:1, 0:128], T.rl[0:1, 0:NL], False, False, [q15, r1, r2])
-    si = scan(T.ii[:, 1:13], T.onef[:, 0:12], T.ct[:, 0:12], ct + [onef, m_ii])
-    mm(T.pf[0:16, 0:2], T.trm[:, 0:16], T.ii[:, 11:13], True, False, [si, trm])
-    p = mm(T.pf[0:16, 0:2], T.eqm[:, 0:16], T.ii[:, me:me + 2], False, True, [eqm, m_ii])
-    rc = ts(T.rc[0:16, 0:NL], T.xc[0:16, 0:NL], T.pf[0:16, 1:2], OP.min, T.pf[0:16, 0:1], OP.max, deps=[p] + xc)
-    p = mm(T.ph[:, 0:NL], T.onef[0:16, 0:128], T.rc[0:16, 0:NL], False, True, [rc])
-    lu = ts(T.lu[:, 0:NL - 1], T.ph[:, 0:NL - 1], T.ph[:, NL - 1:NL], OP.subtract, float(NT - 1), OP.min, deps=[p])
-    if not owner:
-        xs_v = sort_v()
-    for b, d in enumerate(dests):
-        out, win = T.ck[:, CAP * b:CAP * b + CAP], T.xw[:, 0:NT].indirect(T.lu[:, 16 * b:16 * b + 16])
-        c = (cp if b % 2 == 0 else ac)(out, win, [lu, xs_v, xs_s])
-        slot = NT + CAP * (me if me < d else me - 1)
-        write([team_of[d][0]], out, T.xw[:, slot:slot + CAP], T.sem.pin, off, T.sem.loc, loc, [c])
+    xs = [ac(T.xw[:, H:NT], T.xt[:, 0:NT].indirect(T.sl[:, 32:64]), [sl] + x_in),
+          cp(T.xw[:, 0:H], T.xt[:, 0:NT].indirect(T.sl[:, 0:32]), [sl] + x_in)]
 
     if owner:
-        RI, UI, AI, BI = T.oi[:, 0:30], T.oi[:, 32:36], T.oi[:, 36:40], T.oi[:, 40:44]
-        i_ri = iota(RI, [[0, 3], [1, 10]], 0, 0)
-        i_16 = iota(T.c16[:], [[16, 64]], 0, 0, True)
-        ib_ = []
-        if me > 0:
-            ib_.append(iota(ow("bs", 0, me), [[CAP, me]], NT + NT * me, 0, True))
-        if me < NR - 1:
-            ib_.append(iota(ow("bs", me + 1, NR), [[CAP, NR - 1 - me]], NT + NT * me + CAP * me, 0, True))
+        msk, cst = [], ("cst", 3 * noff)
         kb = ms(ow("bs", me, me + 1), float(NT * me))
-        ka = ms(ow("x10", 0, 10), float(NT * me))
-        kx = ms(ow("x10", me, me + 1), 0.0, [ka])
-        r8 = ts(RC8, RC, 8.0, OP.add)
-        k0 = ts(ow("mk0", 0, 30), RI, RC, OP.is_equal, deps=[i_ri])
-        k1 = ts(ow("mk1", 0, 30), RI, RC8, OP.is_equal, deps=[r8])
-        ib = ts(ow("ib", 0, 10), T.onef[:, 0:10], T.ii[:, 10:11], OP.mult, deps=[si])
-        mm(T.pa[:, 0:10], T.trm[:], ow("ib", 0, 10), True, False, [ib])
-        mm(T.pa[:, 0:10], T.eqm[:], T.ii[:, 0:10], False, True)
-        mm(T.pa[:, 10:20], T.eqm[:], T.ct[:, 0:10], True, True, ct)
-        p = mm(T.pa[:, 20:30], T.trm[:], T.ct[:, 0:10], True, True)
-        gn = cp(ow("gnl", 0, 30), T.pa[:, 0:30], [p])
-        G, NN, L = ow("gnl", 0, 10), ow("gnl", 10, 20), ow("gnl", 20, 30)
-        t1 = tt(ow("t1", 0, 10), ow("x10", 0, 10), G, OP.subtract, [gn, kx])
-        c1 = tt(ow("c1", 0, 10), L, G, OP.subtract)
-        t2 = tt(ow("t2", 0, 10), ow("t1", 0, 10), NN, OP.min, [t1])
-        q0 = cp(ow("qq", 0, 10), G)
-        t3 = ts(ow("t3", 0, 10), ow("t2", 0, 10), 0.0, OP.max, deps=[t2])
-        q1 = tt(ow("qq", 10, 20), G, NN, OP.add)
-        c2 = tt(ow("c2", 0, 10), ow("c1", 0, 10), ow("bs", 0, 10), OP.add, [c1, kb] + ib_)
-        p = mm(T.pb[:, 0:10], T.onef[0:16, 0:128], ow("t3", 0, 10, 16), True, True, [t3])
-        q2 = tt(ow("qq", 20, 30), ow("c2", 0, 10), T.pb[:, 0:10], OP.subtract, [p, c2])
-        a0 = tt(ow("qm0", 0, 30), ow("qq", 0, 30), ow("mk0", 0, 30), OP.mult, [q0, q1, q2, k0])
-        a1 = tt(ow("qm1", 0, 30), ow("qq", 0, 30), ow("mk1", 0, 30), OP.mult, [k1])
-        r = []
-        for s, qm, a in ((0, "qm0", a0), (1, "qm1", a1)):
-            r.append(red(ow("sg", 2 * s, 2 * s + 1), ow(qm, 0, 10), [a]))
-            r.append(red(ow("sg", 2 * s + 1, 2 * s + 2), ow(qm, 10, 20)))
-            r.append(red(ow("sv", 2 * s, 2 * s + 1), ow(qm, 20, 30)))
-        u = ts(UI, ow("sg", 0, 4), float(NT * me), OP.subtract, deps=r)
-        n = [ts(ow("sv", 2 * s + 1, 2 * s + 2), ow("sv", 2 * s, 2 * s + 1), -1.0, OP.mult) for s in (0, 1)]
-        ai = ts(AI, UI, 4, OP.arith_shift_right, deps=[u])
-        bi = ts(BI, UI, 15, OP.bitwise_and)
-        af = cp(ow("af", 0, 4), AI, [ai])
-        bf = cp(ow("bf", 0, 4), BI, [bi])
-        mm(T.pi[:, 0:64], T.onef[0:1, 0:128], T.c16[0:1, 0:64], True, False, [i_16])
-        mm(T.pi[:, 0:64], T.q15[0:1, 0:128], T.onef[0:1, 0:64], False, False)
-        for s, e in ((0, 0), (0, 1), (1, 0), (1, 1)):
-            K, o = (128, 32)[s], 2 * s + e
-            A, B, C = [ow(b, o, o + 1, K) for b in ("af", "bf", "sv")]
-            R1, R2, LL = T.ra[0:K, 64 * o:64 * o + 64], T.rb[0:K, 64 * o:64 * o + 64], T.ll[0:K, 128 * o:128 * o + 128]
-            v1 = ts(R1, T.nf[0:K, 0:64], A, OP.is_gt, C, OP.mult, deps=[af, bf] + n)
-            v2 = ts(R2, T.nf[0:K, 0:64], A, OP.is_equal, C, OP.mult)
-            v3 = ts(LL, T.f15[0:K, 0:128], B, OP.is_ge)
-            mm(T.pi[:, 0:64], T.onef[0:K, 0:128], R1, False, False, [v1])
-            p = mm(T.pi[:, 0:64], LL, R2, False, (s, e) == (1, 1), [v2, v3])
+        for s in (0, 1):
+            at = 18 - 8 * s
+            e0 = ts(ow("e0", 0, 12), T.oi[:, at - 1:at + 11], RC, OP.is_equal, deps=[cst, cf] + msk)
+            e1 = ts(ow("e1", 0, 12), T.oi[:, at:at + 12], RC, OP.is_equal)
+            if s == 0:
+                e2 = ts(ow("e2", 0, 12), T.oi[:, at - 10:at + 2], RC, OP.is_equal)
+                e3 = ms(ow("e2", 0, 12, 1), 0.0, [e2])
+                d = tt(ow("wa", 0, 12), ow("e0", 0, 12), ow("e1", 0, 12), OP.subtract, [e0, e1])
+                d = tt(ow("wb", 0, 12), ow("wa", 0, 12), ow("e2", 0, 12), OP.subtract, [d, e3])
+            else:
+                d = tt(ow("wb", 0, 12), ow("e0", 0, 12), ow("e1", 0, 12), OP.subtract, [e0, e1])
+            a1 = cp(T.md[:, 48 * s:48 * s + 10], ow("wb", 1, 11), [d])
+            a2 = ts(T.md[:, 48 * s + 10:48 * s + 20], ow("e1", 1, 11), -1.0, OP.mult)
+            a3 = cp(T.md[:, 48 * s + 31:48 * s + 41], ow("wb", 1, 11))
+            a4 = cp(T.mg[:, 16 * s:16 * s + 11], ow("e0", 1, 12))
+            z1 = [ms(ow("wb", j, j + 1), 0.0, [a1, a3]) for j in (0, me + 1, 11)]
+            a5 = tt(T.md[:, 48 * s + 20:48 * s + 31], ow("wb", 1, 12), ow("wb", 0, 11), OP.subtract, z1)
+            msk += [a1, a2, a3, a4, a5]
+        mm(T.pi[:, 0:64], T.onef[0:1, 0:128], T.c16[0:1, 0:64], True, False, [cst, onef])
+        mm(T.pi[:, 0:64], T.q15[0:1, 0:128], T.onef[0:1, 0:64], False, False, [q15])
+        mm(T.pa[:, 31:41], T.onef[0:1, 0:128], ow("bs", 0, 10, 1), True, True, [kb] + i_bs)
+
+    if collect:
+        ct = [("hin", (NR - 1) * noff)] + own_ct
+        to = [team[t] for t, c in HAND if c == spot]
+        write(to, T.ctl[:], T.ctl[:], T.sem.cin, off, T.sem.loc, loc, ct)
+    else:
+        ct = [("cin", noff)]
+    mm(T.ph[:, 0:NL], T.onef[0:1, 0:128], T.cl[0:1, 0:NL], True, False, [onef, i_cl, cl])
+    mm(T.ph[:, 0:NL], T.q15[0:1, 0:128], T.rl[0:1, 0:NL], False, False, [q15, r1, r2])
+    CT = T.ctl[:, 0:80:8]
+    mm(T.pf[0:w, 0:10], T.trm[:, 0:w], CT, True, True, ct + [trm])
+    p = mm(T.pf[0:w, 10:20], T.eqm[:, 0:w], CT, True, True, [eqm])
+    if owner:
+        ga = red(T.gx[:, 0:1], T.pf[:, 0:10], [p])
+        gx = scan(T.gx[:, 1:11], T.onef[:, 0:10], T.pf[:, 10:20], [ga, onef], T.gx[:, 0:1])
+        G0, G1, gd = T.gx[0:16, me:me + 1], T.gx[0:16, me + 1:me + 2], [gx]
+    else:
+        gd = [red(T.gx[0:16, e:e + 1], T.pf[0:16, 0:10 + me + e], [p]) for e in (0, 1)]
+        G0, G1 = T.gx[0:16, 0:1], T.gx[0:16, 1:2]
+    rc = ts(T.rc[0:16, 0:NL], T.xc[0:16, 0:NL], G1, OP.min, G0, OP.max, deps=gd + xc)
+    pl = mm(T.ph[:, 0:NL], T.onef[0:16, 0:128], T.rc[0:16, 0:NL], False, True, [rc])
+    if owner:
+        mi = ts(ow("mi", 0, 11, 16), T.gx[0:16, 0:11], float(NT * me), OP.min, deps=[gx])
+        mm(T.pa[:, 0:10], T.trm[:], CT, True, True, ct)
+        mm(T.pa[:, 10:20], T.eqm[:], CT, True, True)
+        p_m = mm(T.pa[:, 20:31], T.onef[0:16, 0:128], ow("mi", 0, 11, 16), True, True, [mi])
+        gs = [tt(ow("gs", 16 * s, 16 * s + 11), T.gx[:, 0:11], T.mg[:, 16 * s:16 * s + 11], OP.mult, msk) for s in (0, 1)]
+    lu = ts(T.lu[:, 0:NL - 1], T.ph[:, 0:NL - 1], T.ph[:, NL - 1:NL], OP.subtract, float(NT - 1), OP.min, deps=[pl])
+    for b, (d, lo, hi) in enumerate(dests):
+        mid, o = (lo + hi) // 2, CAP * b
+        c = [f(T.ck[:, o + u:o + v], T.xw[:, 0:NT].indirect(T.lu[:, (o + u) // 16:(o + v) // 16]), [lu] + xs)
+             for u, v, f in ((lo, mid, ac), (mid, hi, cp))]
+        slot = NT + CAP * (me if me < d else me - 1)
+        write([team_of[d][0]], T.ck[:, o + lo:o + hi], T.xw[:, slot + lo:slot + hi], T.sem.pin, off, T.sem.loc, loc, c)
+
+    if owner:
+        gr = [red(ow("sg", s, s + 1), ow("gs", 16 * s, 16 * s + 11), gs) for s in (0, 1)]
+        pr = [tt(T.pr[:, 48 * s:48 * s + 41], T.pa[:, 0:41], T.md[:, 48 * s:48 * s + 41], OP.mult, [p_m]) for s in (0, 1)]
+        gi = cp(T.oi[:, 32:34], ow("sg", 0, 2), gr)
+        dr = [red(ow("sv", s, s + 1), T.pr[:, 48 * s:48 * s + 41], pr) for s in (0, 1)]
+        bi = ts(T.oi[:, 36:38], T.oi[:, 32:34], 15, OP.bitwise_and, deps=[gi])
+        v = {}
+        for s in (0, 1):
+            K = (128, 32)[s]
+            G, C = [ow(b, s, s + 1, K) for b in ("sg", "sv")]
+            for e, at in ((0, 65), (1, 64)):
+                v[s, e] = ts(T.ra[0:K, 128 * s + 64 * e:128 * s + 64 * e + 64], T.c16[0:K, at:at + 64], G, OP.is_gt, C, OP.mult, deps=dr)
+            if s == 0:
+                bf = cp(ow("bf", 0, 2), T.oi[:, 36:38], [bi])
+        for s in (0, 1):
+            K = (128, 32)[s]
+            for e, cmp in ((0, OP.is_ge), (1, OP.is_lt)):
+                L = T.ll[0:K, 256 * s + 128 * e:256 * s + 128 * e + 128]
+                l = ts(L, T.f15[0:K, 0:128], ow("bf", s, s + 1, K), cmp, deps=[bf])
+                p = mm(T.pi[:, 0:64], L, T.ra[0:K, 128 * s + 64 * e:128 * s + 64 * e + 64], False, (s, e) == (1, 1), [l, v[s, e]])
         yu = cp(T.yu[:], T.pi[:, 0:64], [p])
-        ready = [yu, xs_v, xs_s, ("pin", (NR - 1) * noff), ("rep", rep[0])]
-        pc = {}
-        for b, f in ((0, cp), (2, ac), (1, cp), (3, ac)):
-            pc[b] = f(T.xt[:, CAP * b:CAP * b + CAP], T.xw[:, 0:NT + 9 * CAP].indirect(T.yu[:, 16 * b:16 * b + 16]), ready)
-        for b, q in ((0, "y"), (2, "y"), (1, "y"), (3, "s")):
-            eng = g.sync if q == "y" else g.scalar
-            op(q, lambda eng=eng, b=b: eng.dma_start(T.y[:, CAP * b:CAP * b + CAP], T.xt[:, CAP * b:CAP * b + CAP]), [pc[b]], 16)
+        ready = [yu] + xs + [("pin", (NR - 1 + (me in plan["half"])) * noff), ("rep", rep[0])]
+        pieces, at = [], 0
+        for q, n in PIECES:
+            f = cp if q == "v" else ac
+            pieces.append((f(T.xt[:, at:at + n], T.xw[:, 0:NT + 9 * CAP].indirect(T.yu[:, at // 16:(at + n) // 16]), ready), at, n))
+            at += n
+        for j, (d, at, n) in enumerate(pieces):
+            last = j == len(pieces) - 1
+            eng = g.scalar if last else g.sync
+            op("s" if last else "y", lambda eng=eng, at=at, n=n: eng.dma_start(T.y[:, at:at + n], T.xt[:, at:at + n]), [d], 16)
 
     queue = {"g": g, "v": V, "t": E, "s": S, "y": g.sync}
     needed = set(d for o in ops for d in o[2] if isinstance(d, int)) | set(i for i, o in enumerate(ops) if o[3] == 16)

import numpy as np
from concourse.bass import DstId, RemoteDMATransfer
from concourse.mybir import AluOpType, AxisListType, ActivationFunctionType

WORLD = 256
NR, NT, CAP = 10, 1024, 256
NEV = 141


def _sb(n, dtype="float32"):
    return ("sbuf", [128, n], dtype)


_SMALL = ["bs", "e0", "e1", "e2", "wa", "wb", "mi", "gs", "sg", "sv", "bf"]
_AT = {n: 32 * k for k, n in enumerate(_SMALL)}
COLLECT = (1, 2)
HAND = ((0, 1), (3, 2))
SHARE = (0, 7, 13, 18)
SLOTS = [(0, 0), (0, 1), (1, 0), (1, 1), (1, 2), (2, 0), (2, 1), (3, 0), (3, 1)]
LATE = (1.6, 0.0, 0.1, 1.6)
OWN, CUT = 2, 4
PIECES = (("v", 128), ("s", 128), ("v", 384), ("s", 384))

SCRATCH = {
    "k1": _sb(8, "int32"),
    "xt": _sb(NT),
    "xw": _sb(NT + 9 * CAP),
    "ck": _sb(3 * CAP),
    "hs": _sb(8, "bfloat16"),
    "ctl": _sb(80, "bfloat16"),
    "ci": _sb(64, "int32"), "cf": _sb(10), "l8": _sb(8, "uint16"), "l9": _sb(10, "uint16"),
    "nf": _sb(144, "int32"), "f7": _sb(144, "int32"), "f15": _sb(144, "int32"), "kk": _sb(128),
    "geq": _sb(128, "bfloat16"), "nge": _sb(128, "bfloat16"), "mge": _sb(128, "bfloat16"),
    "mlt": _sb(128, "bfloat16"), "mgt": _sb(128, "bfloat16"), "idn": _sb(128, "bfloat16"),
    "sel": _sb(8), "bm": _sb(144, "bfloat16"),
    "lo": _sb(128), "lo2": _sb(128), "hi2": _sb(128), "dd": _sb(128, "bfloat16"), "zb": _sb(256, "bfloat16"),
    "oneb": _sb(128, "bfloat16"), "onef": _sb(128), "q15": _sb(128), "trm": _sb(128, "bfloat16"), "eqm": _sb(128, "bfloat16"),
    "xc": _sb(64), "cl": _sb(64), "rl": _sb(64), "c16": _sb(144),
    "oh": _sb(128, "bfloat16"), "rse": _sb(144, "bfloat16"), "rxx": _sb(144, "bfloat16"),
    "oht": _sb(128), "zt": _sb(128), "pu": _sb(8, "uint16"), "wb": _sb(NT, "bfloat16"), "sl": _sb(64, "uint16"),
    "gx": _sb(32), "rc": _sb(64), "lu": _sb(64, "uint16"),
    "ow": _sb(32 * len(_SMALL)), "oi": _sb(48, "int32"), "md": _sb(96), "mg": _sb(32), "pr": _sb(96), "ra": _sb(256), "ll": _sb(512),
    "yu": _sb(64, "uint16"),
    "pa": ("psum", [128, 512], "float32"), "pb": ("psum", [128, 512], "float32"), "pc": ("psum", [128, 512], "float32"),
    "pd": ("psum", [128, 512], "float32"), "pe": ("psum", [128, 512], "float32"), "pf": ("psum", [128, 512], "float32"),
    "ph": ("psum", [128, 512], "float32"), "pi": ("psum", [128, 512], "float32"),
}
SEMAPHORES = ["kin", "xin", "hin", "cin", "pin", "cst", "loc", "rep"] + ["e%d" % i for i in range(NEV)]

_CACHE = {}


def _make_plan(T, topo):
    cores = list(T.cores)
    place = lambda c: (topo.host(c), topo.chip(c))
    team = []
    for o in cores:
        cou = [c for c in range(WORLD) if place(c) == place(o) and c != o
               and all(topo.may_write(c, d) for d in cores if d != o)]
        near = [c for c in cou if topo.die(c) == topo.die(o)]
        far = [c for c in cou if topo.die(c) != topo.die(o)]
        team.append([o, near[0], far[0], far[1]])
    mate = [next(m for m in range(WORLD) if topo.mates(o, m)) for o in cores]
    same = lambda s, d: topo.same_plane(cores[s], cores[d])

    def links(s, d, die):
        a, b = cores[s], cores[d]
        if same(s, d):
            return [("out", place(a), die), ("in", place(b), die)]
        if topo.mates(a, b):
            return [("mate", place(a), die)]
        return [("mate", place(a), die), ("out", place(mate[s]), die), ("in", place(b), die)]

    LK = {(s, d, e): links(s, d, e) for s in range(NR) for d in range(NR) if s != d for e in (0, 1)}
    TIME = {"out": 0.85, "in": 1.0, "mate": 1.0}
    start = [LATE[c] + 0.25 * i for c, i in SLOTS]
    seq = sorted(range(9), key=lambda p: start[p])
    alone = [d for d in range(NR) if not any(topo.mates(cores[d], c) for c in cores)]

    def cost(B, half):
        free, last = {}, [0.0] * NR
        for p in seq:
            for s in range(NR):
                d = B[s][p]
                parts = [(start[p], SLOTS[p][0], 1.0)]
                if p == CUT and half.get(d) == s:
                    parts = [(start[p], 1, 0.5), (start[p] + 0.25, 2, 0.5)]
                for st, c, z in parts:
                    end = free[s, c] = max(free.get((s, c), 0.0), st) + 0.9 * z
                    for l in LK[s, d, 0 if c < 2 else 1]:
                        free[l] = max(free.get(l, 0.0), st) + TIME[l[0]] * z
                        end = max(end, free[l])
                    last[d] = max(last[d], end)
        return sum(t ** 16 for t in free.values()) + sum(t ** 16 for t in last)

    def fits(s, row, half):
        return all(same(s, d) for d in row[:OWN]) and all(row[CUT] == d for d in half if half[d] == s)

    best = None
    for shift in range(8):
        half = {d: (d + 1 + shift) % NR for d in alone}
        B = []
        for s in range(NR):
            rot = [(s + k) % NR for k in range(1, NR)]
            cut = [d for d in rot if half.get(d) == s]
            own = [d for d in rot if same(s, d) and d not in cut][:OWN]
            row = own + [d for d in rot if d not in own + cut]
            B.append(row[:CUT] + cut + row[CUT:])
        now, again = cost(B, half), True
        while again:
            again = False
            for s in range(NR):
                row = B[s]
                for p in range(9):
                    for q in range(p + 1, 9):
                        row[p], row[q] = row[q], row[p]
                        c = cost(B, half) if fits(s, row, half) else now
                        if c < now:
                            now, again = c, True
                        else:
                            row[p], row[q] = row[q], row[p]
        if best is None or now < best[0]:
            best = (now, [list(row) for row in B], half)
    half = best[2]
    carry = []
    for s, row in enumerate(best[1]):
        cut = [d for d in half if half[d] == s]
        c4 = [[(row[p], 0, CAP // 2 if row[p] in cut else CAP) for p in range(9) if SLOTS[p][0] == c] for c in range(4)]
        c4[2] += [(d, CAP // 2, CAP) for d in cut]
        carry.append(c4)
    return {"team": team, "carry": carry, "half": half}


def rank_program(g, core, T, topo):
    if "plan" not in _CACHE:
        _CACHE["plan"] = _make_plan(T, topo)
    plan = _CACHE["plan"]
    team_of = plan["team"]
    me = next((r for r in range(NR) if core in team_of[r]), None)
    if me is None:
        return
    team = team_of[me]
    spot = team.index(core)
    owner, collect = spot == 0, spot in COLLECT
    dests = plan["carry"][me][spot]
    ND = len(dests)
    NL = 16 * ND + 1
    OP, AX, COPY = AluOpType, AxisListType.X, ActivationFunctionType.Copy
    V, S, E = g.vector, g.scalar, g.tensor

    ops = []

    def op(q, fn, deps=(), inc=1):
        ops.append((q, fn, list(deps), inc))
        return len(ops) - 1

    def ts(out, in0, s1, op0, s2=None, op1=None, deps=()):
        if op1 is None:
            return op("v", lambda: V.tensor_scalar(out=out, in0=in0, scalar1=s1, scalar2=None, op0=op0), deps)
        return op("v", lambda: V.tensor_scalar(out=out, in0=in0, scalar1=s1, scalar2=s2, op0=op0, op1=op1), deps)

    def tt(out, a, b, o, deps=()):
        return op("v", lambda: V.tensor_tensor(out=out, in0=a, in1=b, op=o), deps)

    def scan(out, a, b, deps=(), initial=0.0):
        return op("v", lambda: V.tensor_tensor_scan(out=out, data0=a, data1=b, initial=initial, op0=OP.mult, op1=OP.add), deps)

    def cp(out, a, deps=()):
        return op("v", lambda: V.tensor_copy(out=out, in_=a), deps)

    def ac(out, a, deps=()):
        return op("s", lambda: S.activation(out=out, in_=a, func=COPY), deps)

    def ms(a, v, deps=()):
        return op("v", lambda: V.memset(a, v), deps)

    def red(out, a, deps=()):
        return op("v", lambda: V.tensor_reduce(out=out, in_=a, axis=AX, op=OP.add), deps)

    def mm(out, l, r, start, stop, deps=()):
        return op("t", lambda: E.matmul(out=out, lhsT=l, rhs=r, start=start, stop=stop), deps)

    def iota(out, pattern, base, mult, small=False):
        if small:
            return op("g", lambda: g.iota(out, pattern, base, mult, allow_small_or_imprecise_dtypes=True))
        return op("g", lambda: g.iota(out, pattern, base, mult))

    def ow(name, a, b, k=128):
        return T.ow[0:k, _AT[name] + a:_AT[name] + b]

    loc, rep = [0], [0]

    def write(targets, src, dst, sem, mask, lsem, count, deps=()):
        ids = [topo.addr(t, core) for t in targets]
        count[0] += bin(mask).count("1")
        if len(targets) == 1:
            rid, pid = ids[0]
            return op("g", lambda: g.remote_dma(out_ap=dst, in_ap=src, remote_sem=sem, local_sem=lsem, pid=pid, routing_id=rid,
                                                dma_engine_mask=mask), deps, 0)
        tr = [RemoteDMATransfer(dst_ids=[DstId(rid=r, pnc=p) for r, p in ids], dma_engine_mask=mask, remote_sem=sem,
                                srcs=[src], dsts=[dst] * len(targets))]
        return op("g", lambda: g.remote_dma_fused(tr, local_sem=lsem), deps, 0)

    off = topo.mask(team[1], next(c for c in T.cores if c != team[0]))
    noff = bin(off).count("1")
    onc = [topo.mask(team[0], h) for h in team[1:]]
    H = NT // 2

    if owner:
        k_in = op("y", lambda: g.sync.dma_start(T.k1[:], T.key[:]), (), 16)
        x_in = [op("y", lambda: g.sync.dma_start(T.xt[:, 0:H], T.x[:, 0:H]), (), 16),
                op("y", lambda: g.sync.dma_start(T.xt[:, H:NT], T.x[:, H:NT]), (), 16)]
    else:
        k_in, x_in = ("kin", noff), [("xin", 2 * bin(onc[spot - 1]).count("1"))]

    i_p = iota(T.ci[:, 0:1], [[1, 1]], 0, 1)
    i_8 = iota(T.ci[:, 8:16], [[0, 8]], 0, 1)
    i_nf = iota(T.nf[:], [[1, 144]], 0, 0)
    i_kk = iota(T.kk[:], [[1, 16], [0, 8]], 0, 0, True)
    i_9 = iota(T.ci[:, 24:33], [[16, 9]], 7, 0)
    i_lo = iota(T.lo[:], [[16, 8], [1, 2], [0, 8]], 0, 0, True)
    if owner:
        write(team[1:], T.k1[:], T.k1[:], T.sem.kin, off, T.sem.loc, loc, [k_in])
        for h, m in zip(team[1:], onc):
            for a, xd in ((0, x_in[0]), (H, x_in[1])):
                write([h], T.xt[:, a:a + H], T.xt[:, a:a + H], T.sem.xin, m, T.sem.rep, rep, [xd])
    else:
        tab, pat, base = ((T.oi[:, 0:32], [[1, 32]], -18), (T.c16[:, 0:64], [[16, 64]], 0), (T.c16[:, 64:129], [[16, 65]], NT * me))[spot - 1]
        write([team[0]], tab, tab, T.sem.cst, off, T.sem.loc, loc, [iota(tab, pat, base, 0, spot > 1)])
    i_cl = iota(T.cl[:, 0:16 * ND], [[0, ND], [16, 16]], 0, 0, True)
    if owner:
        i_bs = []
        if me > 0:
            i_bs.append(iota(ow("bs", 0, me), [[CAP, me]], NT + NT * me, 0, True))
        if me < NR - 1:
            i_bs.append(iota(ow("bs", me + 1, NR), [[CAP, NR - 1 - me]], NT + NT * me + CAP * me, 0, True))

    m_one = ms(T.oneb[:], 1.0)
    m_z = ms(T.zb[:], 0.0)
    m_w = [ac(T.wb[:, 256 * j:256 * j + 256], T.zb[:], [m_z]) for j in range(4)]
    m_rse = ms(T.rse[:], 0.0)
    l8i = ts(T.ci[:, 16:24], T.ci[:, 8:16], 7, OP.bitwise_and, deps=[i_8])
    c1 = ts(T.ci[:, 1:2], T.ci[:, 0:1], 7, OP.bitwise_and, deps=[i_p])
    c2 = ts(T.ci[:, 2:3], T.ci[:, 0:1], 15, OP.bitwise_and)
    c3 = ts(T.ci[:, 3:4], T.ci[:, 0:1], 3, OP.logical_shift_right)
    c4 = ts(T.ci[:, 4:5], T.ci[:, 0:1], 8, OP.bitwise_and)
    c5 = ts(T.ci[:, 5:6], T.ci[:, 0:1], 4, OP.logical_shift_right)
    l8 = cp(T.l8[:], T.ci[:, 16:24], [l8i])
    cf = cp(T.cf[:, 0:6], T.ci[:, 0:6], [c1, c2, c3, c4, c5])
    PC, GC, QC, KC, EC, RC, M0, M1 = [T.cf[:, j:j + 1] for j in range(8)]
    m0 = ts(M0, QC, 0.0, OP.is_equal, deps=[cf])
    m1 = ts(M1, QC, 1.0, OP.is_equal)
    f7 = ts(T.f7[:], T.nf[:], 7, OP.bitwise_and, deps=[i_nf])
    f15 = ts(T.f15[:], T.nf[:], 15, OP.bitwise_and)
    F7, F15 = T.f7[:, 0:128], T.f15[:, 0:128]
    geq = ts(T.geq[:], F7, GC, OP.is_equal, deps=[f7])
    nge = ts(T.nge[:], T.nf[:, 0:128], PC, OP.is_le, -1.0, OP.mult)
    l9 = ts(T.l9[:, 0:9], T.ci[:, 24:33], EC, OP.add, deps=[i_9])

    def one_hot():
        return op("v", lambda: V.tensor_tensor(out=T.oh[:], in0=T.k1[:, 0:8].indirect(T.l8[:, 0:8]), in1=T.kk[:], op=OP.is_equal),
                  [k_in, l8, i_kk])

    def sort_constants():
        mlt = ts(T.mlt[:], F7, GC, OP.is_gt)
        mgt = ts(T.mgt[:], F7, GC, OP.is_lt)
        idn = ts(T.idn[:], T.nf[:, 0:128], PC, OP.is_equal)
        mge = tt(T.mge[:], T.geq[:], T.nge[:], OP.mult, [geq, nge])
        sel = ts(T.sel[:], T.f7[:, 0:8], GC, OP.is_equal)
        return mlt, mgt, idn, mge, sel

    def scatter_constants():
        bm = ts(T.bm[:], T.f15[:], 0.0, OP.is_equal, deps=[f15])
        hi2 = ts(T.hi2[:], F7, M1, OP.mult, 128.0, OP.mult, deps=[m1])
        lo2 = ts(T.lo2[:], T.lo[:], KC, OP.add, M0, OP.mult, deps=[i_lo, m0])
        dd = tt(T.dd[:], T.lo2[:], T.hi2[:], OP.add, [lo2, hi2])
        return bm, dd

    if owner:
        oh = one_hot()
        mlt, mgt, idn, mge, sel = sort_constants()
    else:
        mlt, mgt, idn, mge, sel = sort_constants()
        bm, dd = scatter_constants()
        oh = one_hot()
        p = mm(T.pa[:, 0:8], T.oh[:], T.oneb[:, 0:8], True, True, [oh, m_one])
        hist = cp(T.hs[:], T.pa[:, 0:8], [p])
        cols = [((me + k) % NR, c) for k in range(1, NR) for c in COLLECT]
        write([team_of[d][c] for d, c in cols[SHARE[spot - 1]:SHARE[spot]]], T.hs[:], T.ctl[:, 8 * me:8 * me + 8], T.sem.hin, off,
              T.sem.loc, loc, [hist])

    rs = scan(T.rse[:, 8:136], T.oneb[:], T.oh[:], [oh, m_one, m_rse])
    own_ct = [cp(T.ctl[:, 8 * me:8 * me + 8], T.hs[:], [hist])] if collect else []
    rx = cp(T.rxx[:], T.rse[:, 0:144].indirect(T.l9[:, 0:9]), [rs, l9])
    if owner:
        bm, dd = scatter_constants()
    po = mm(T.pb[:, 0:128], T.oh[:], T.idn[:], True, True, [oh, idn])
    oht = ac(T.oht[:], T.pb[:, 0:128], [po])
    mm(T.pc[:, 0:128], T.oh[:], T.mge[:], True, False, [mge])
    mm(T.pc[:, 0:128], T.rse[:, 8:136], T.geq[:], False, False, [rs, geq])
    mm(T.pc[:, 0:128], T.rxx[:, 8:136], T.mlt[:], False, False, [rx, mlt])
    p = mm(T.pc[:, 0:128], T.rxx[:, 0:128], T.mgt[:], False, True, [mgt])
    z = tt(T.zt[:], T.pc[:, 0:128], T.oht[:], OP.mult, [p, oht])
    p = mm(T.pd[:, 0:8], T.zt[:], T.sel[:], True, True, [z, sel])
    pu = cp(T.pu[:], T.pd[:, 0:8], [p])
    sc = cp(T.wb[:, 0:NT].indirect(T.pu[:, 0:8]), T.dd[:], [pu, dd] + m_w)
    for i in range(16):
        p = mm(T.pe[:, 0:64], T.bm[:, 16 - i:144 - i], T.wb[:, i:NT:16], i == 0, i == 15, [sc, bm])
    w = 128 if owner else 16
    onef = ms(T.onef[:], 1.0)
    trm = ts(T.trm[:, 0:w], T.f15[:, 0:w], KC, OP.is_gt)
    eqm = ts(T.eqm[:, 0:w], T.f15[:, 0:w], KC, OP.is_equal)
    q15 = cp(T.q15[:], F15)
    xc = [ms(T.xc[:, 16 * b:16 * b + 16], float(NT * d)) for b, (d, _, _) in enumerate(dests)] + [ms(T.xc[:, NL - 1:NL], 0.0)]
    cl = ms(T.cl[:, NL - 1:NL], 0.0)
    r1 = ms(T.rl[:, 0:NL - 1], 1.0)
    r2 = ms(T.rl[:, NL - 1:NL], 0.0)
    sl = cp(T.sl[:], T.pe[:, 0:64], [p])
    xs = [ac(T.xw[:, H:NT], T.xt[:, 0:NT].indirect(T.sl[:, 32:64]), [sl] + x_in),
          cp(T.xw[:, 0:H], T.xt[:, 0:NT].indirect(T.sl[:, 0:32]), [sl] + x_in)]

    if owner:
        msk, cst = [], ("cst", 3 * noff)
        kb = ms(ow("bs", me, me + 1), float(NT * me))
        for s in (0, 1):
            at = 18 - 8 * s
            e0 = ts(ow("e0", 0, 12), T.oi[:, at - 1:at + 11], RC, OP.is_equal, deps=[cst, cf] + msk)
            e1 = ts(ow("e1", 0, 12), T.oi[:, at:at + 12], RC, OP.is_equal)
            if s == 0:
                e2 = ts(ow("e2", 0, 12), T.oi[:, at - 10:at + 2], RC, OP.is_equal)
                e3 = ms(ow("e2", 0, 12, 1), 0.0, [e2])
                d = tt(ow("wa", 0, 12), ow("e0", 0, 12), ow("e1", 0, 12), OP.subtract, [e0, e1])
                d = tt(ow("wb", 0, 12), ow("wa", 0, 12), ow("e2", 0, 12), OP.subtract, [d, e3])
            else:
                d = tt(ow("wb", 0, 12), ow("e0", 0, 12), ow("e1", 0, 12), OP.subtract, [e0, e1])
            a1 = cp(T.md[:, 48 * s:48 * s + 10], ow("wb", 1, 11), [d])
            a2 = ts(T.md[:, 48 * s + 10:48 * s + 20], ow("e1", 1, 11), -1.0, OP.mult)
            a3 = cp(T.md[:, 48 * s + 31:48 * s + 41], ow("wb", 1, 11))
            a4 = cp(T.mg[:, 16 * s:16 * s + 11], ow("e0", 1, 12))
            z1 = [ms(ow("wb", j, j + 1), 0.0, [a1, a3]) for j in (0, me + 1, 11)]
            a5 = tt(T.md[:, 48 * s + 20:48 * s + 31], ow("wb", 1, 12), ow("wb", 0, 11), OP.subtract, z1)
            msk += [a1, a2, a3, a4, a5]
        mm(T.pi[:, 0:64], T.onef[0:1, 0:128], T.c16[0:1, 0:64], True, False, [cst, onef])
        mm(T.pi[:, 0:64], T.q15[0:1, 0:128], T.onef[0:1, 0:64], False, False, [q15])
        mm(T.pa[:, 31:41], T.onef[0:1, 0:128], ow("bs", 0, 10, 1), True, True, [kb] + i_bs)

    if collect:
        ct = [("hin", (NR - 1) * noff)] + own_ct
        to = [team[t] for t, c in HAND if c == spot]
        write(to, T.ctl[:], T.ctl[:], T.sem.cin, off, T.sem.loc, loc, ct)
    else:
        ct = [("cin", noff)]
    mm(T.ph[:, 0:NL], T.onef[0:1, 0:128], T.cl[0:1, 0:NL], True, False, [onef, i_cl, cl])
    mm(T.ph[:, 0:NL], T.q15[0:1, 0:128], T.rl[0:1, 0:NL], False, False, [q15, r1, r2])
    CT = T.ctl[:, 0:80:8]
    mm(T.pf[0:w, 0:10], T.trm[:, 0:w], CT, True, True, ct + [trm])
    p = mm(T.pf[0:w, 10:20], T.eqm[:, 0:w], CT, True, True, [eqm])
    if owner:
        ga = red(T.gx[:, 0:1], T.pf[:, 0:10], [p])
        gx = scan(T.gx[:, 1:11], T.onef[:, 0:10], T.pf[:, 10:20], [ga, onef], T.gx[:, 0:1])
        G0, G1, gd = T.gx[0:16, me:me + 1], T.gx[0:16, me + 1:me + 2], [gx]
    else:
        gd = [red(T.gx[0:16, e:e + 1], T.pf[0:16, 0:10 + me + e], [p]) for e in (0, 1)]
        G0, G1 = T.gx[0:16, 0:1], T.gx[0:16, 1:2]
    rc = ts(T.rc[0:16, 0:NL], T.xc[0:16, 0:NL], G1, OP.min, G0, OP.max, deps=gd + xc)
    pl = mm(T.ph[:, 0:NL], T.onef[0:16, 0:128], T.rc[0:16, 0:NL], False, True, [rc])
    if owner:
        mi = ts(ow("mi", 0, 11, 16), T.gx[0:16, 0:11], float(NT * me), OP.min, deps=[gx])
        mm(T.pa[:, 0:10], T.trm[:], CT, True, True, ct)
        mm(T.pa[:, 10:20], T.eqm[:], CT, True, True)
        p_m = mm(T.pa[:, 20:31], T.onef[0:16, 0:128], ow("mi", 0, 11, 16), True, True, [mi])
        gs = [tt(ow("gs", 16 * s, 16 * s + 11), T.gx[:, 0:11], T.mg[:, 16 * s:16 * s + 11], OP.mult, msk) for s in (0, 1)]
    lu = ts(T.lu[:, 0:NL - 1], T.ph[:, 0:NL - 1], T.ph[:, NL - 1:NL], OP.subtract, float(NT - 1), OP.min, deps=[pl])
    for b, (d, lo, hi) in enumerate(dests):
        mid, o = (lo + hi) // 2, CAP * b
        c = [f(T.ck[:, o + u:o + v], T.xw[:, 0:NT].indirect(T.lu[:, (o + u) // 16:(o + v) // 16]), [lu] + xs)
             for u, v, f in ((lo, mid, ac), (mid, hi, cp))]
        slot = NT + CAP * (me if me < d else me - 1)
        write([team_of[d][0]], T.ck[:, o + lo:o + hi], T.xw[:, slot + lo:slot + hi], T.sem.pin, off, T.sem.loc, loc, c)

    if owner:
        gr = [red(ow("sg", s, s + 1), ow("gs", 16 * s, 16 * s + 11), gs) for s in (0, 1)]
        pr = [tt(T.pr[:, 48 * s:48 * s + 41], T.pa[:, 0:41], T.md[:, 48 * s:48 * s + 41], OP.mult, [p_m]) for s in (0, 1)]
        gi = cp(T.oi[:, 32:34], ow("sg", 0, 2), gr)
        dr = [red(ow("sv", s, s + 1), T.pr[:, 48 * s:48 * s + 41], pr) for s in (0, 1)]
        bi = ts(T.oi[:, 36:38], T.oi[:, 32:34], 15, OP.bitwise_and, deps=[gi])
        v = {}
        for s in (0, 1):
            K = (128, 32)[s]
            G, C = [ow(b, s, s + 1, K) for b in ("sg", "sv")]
            for e, at in ((0, 65), (1, 64)):
                v[s, e] = ts(T.ra[0:K, 128 * s + 64 * e:128 * s + 64 * e + 64], T.c16[0:K, at:at + 64], G, OP.is_gt, C, OP.mult, deps=dr)
            if s == 0:
                bf = cp(ow("bf", 0, 2), T.oi[:, 36:38], [bi])
        for s in (0, 1):
            K = (128, 32)[s]
            for e, cmp in ((0, OP.is_ge), (1, OP.is_lt)):
                L = T.ll[0:K, 256 * s + 128 * e:256 * s + 128 * e + 128]
                l = ts(L, T.f15[0:K, 0:128], ow("bf", s, s + 1, K), cmp, deps=[bf])
                p = mm(T.pi[:, 0:64], L, T.ra[0:K, 128 * s + 64 * e:128 * s + 64 * e + 64], False, (s, e) == (1, 1), [l, v[s, e]])
        yu = cp(T.yu[:], T.pi[:, 0:64], [p])
        ready = [yu] + xs + [("pin", (NR - 1 + (me in plan["half"])) * noff), ("rep", rep[0])]
        pieces, at = [], 0
        for q, n in PIECES:
            f = cp if q == "v" else ac
            pieces.append((f(T.xt[:, at:at + n], T.xw[:, 0:NT + 9 * CAP].indirect(T.yu[:, at // 16:(at + n) // 16]), ready), at, n))
            at += n
        for j, (d, at, n) in enumerate(pieces):
            last = j == len(pieces) - 1
            eng = g.scalar if last else g.sync
            op("s" if last else "y", lambda eng=eng, at=at, n=n: eng.dma_start(T.y[:, at:at + n], T.xt[:, at:at + n]), [d], 16)

    queue = {"g": g, "v": V, "t": E, "s": S, "y": g.sync}
    needed = set(d for o in ops for d in o[2] if isinstance(d, int)) | set(i for i, o in enumerate(ops) if o[3] == 16)
    event, seen, waited = {}, {q: set() for q in queue}, set()

    def wait(q, d):
        if d in seen[q]:
            return
        seen[q].add(d)
        waited.add(d)
        if isinstance(d, int):
            queue[q].wait_ge(event[d][0], event[d][1])
        else:
            queue[q].wait_ge(T.sem[d[0]], d[1])

    for i, (q, fn, deps, inc) in enumerate(ops):
        for d in deps:
            wait(q, d)
        ins = fn()
        if i in needed:
            event[i] = (T.sem["e%d" % len(event)], inc)
            ins.then_inc(event[i][0], inc)
    for i in sorted(event):
        if i not in waited:
            wait("g", i)
    wait("g", ("loc", loc[0]))
    if owner:
        wait("g", ("rep", rep[0]))
